import numpy as np
import ml_dtypes


def mxq(x, axis, fmt="e4m3"):
    dtype, down = {"e4m3": (ml_dtypes.float8_e4m3fn, 7), "e5m2": (ml_dtypes.float8_e5m2, 14)}[fmt]
    v = np.moveaxis(np.asarray(x, np.float32).astype(ml_dtypes.bfloat16).astype(np.float64), axis, -1)
    blocks = v.reshape(v.shape[:-1] + (-1, 32))
    amax = np.abs(blocks).max(-1, keepdims=True)
    byte = np.maximum(np.where(amax > 0, np.frexp(amax)[1] - 1 + 127, 0) - down, 1)
    scale = np.exp2(byte - 127.0)
    codes = (blocks / scale).astype(np.float32).astype(dtype).astype(np.float64)
    return np.moveaxis((codes * scale).reshape(v.shape), -1, axis)


WIDE = False


def mx_kscale(k):
    if not WIDE:
        return np.ones(k)
    levels = np.array([10, -10, 5, -5, 0])
    if k % 512:
        return np.exp2(np.random.permutation(np.resize(levels, k // 32))).repeat(32)
    a = np.empty((k // 512, 16))
    for p in range(k // 512):
        a[p, :8] = np.random.permutation(np.resize(levels, 8))
        for g in range(8):
            far = levels[np.abs(levels - a[p, g]) >= 10]
            a[p, g + 8] = far[np.random.randint(len(far))]
    return np.exp2(a.ravel()).repeat(32)


def f64(x):
    return np.asarray(x).astype(np.float64)


def striped(idx):
    return np.tile(np.asarray(idx).reshape(-1, 16).T, (8, 1)).astype(np.uint16)


def unstriped(offs):
    return offs[:16].T.reshape(-1).astype(np.int64)


B, N, T, D, DV, NQ = 1, 1024, 2048, 512, 256, 256
CAP = 2.0


def setup_inputs():
    n = np.random.standard_normal
    idx = np.random.permutation(T)[:B * N]
    s = mx_kscale(D)[:, None]
    u = np.ones(T)
    u[idx] = mx_kscale(B * N)
    r = np.random.uniform(0.5, 2.0, T)
    k = n((D, T)) / s
    v = n((DV, T)) / (u * r)
    return {
        "qT": (n((B, D, NQ)) * s * (1.00 / np.sqrt(D))).astype(np.float32),
        "kT": k.astype(np.float32),
        "vT": v.astype(np.float32),
        "vs": np.tile(u * r, (128, 1)).astype(np.float32),
        "og": n((B, NQ, DV)).astype(np.float32),
        "offs": striped(idx),
    }


def reference(qT, kT, vT, vs, og, offs):
    idx = unstriped(offs)
    k = f64(kT)
    v = f64(vT)
    pick = lambda x: x[:, idx].reshape(x.shape[0], B, N).transpose(1, 0, 2)
    q = f64(qT)
    score = mxq(q, 1, "e4m3").transpose(0, 2, 1) @ mxq(pick(k), 1, "e4m3")
    score = CAP * np.tanh(score / CAP)
    m = score.max(-1, keepdims=True)
    p = np.exp(score - m)
    total = p.sum(-1, keepdims=True)
    w = p * pick(f64(vs))[:, :1, :]
    y = mxq(w, 2, "e4m3") @ mxq(pick(v).transpose(0, 2, 1), 1, "e4m3")
    y = y / total
    y = y / (1.0 + np.exp(-f64(og)))
    return y

@@ -1,0 +1,268 @@
+from contextlib import ExitStack
+
+import concourse.mybir as mybir
+from concourse.masks import make_identity
+
+P = 128
+NQ, D, DV, T, N = 256, 512, 256, 2048, 1024
+HALF = 512
+QT = NQ // P
+FLOPS = 2 * NQ * N * (D + DV)
+
+F32 = mybir.dt.float32
+BF16 = mybir.dt.bfloat16
+U32 = mybir.dt.uint32
+U16 = mybir.dt.uint16
+U8 = mybir.dt.uint8
+FP8X4 = mybir.dt.float8_e4m3fn_x4
+ACT = mybir.ActivationFunctionType
+ALU = mybir.AluOpType
+AX = mybir.AxisListType
+
+
+def tile_attend_x_cap_gate_topk_kernel(tc, qT, kT, vT, vs, og, offs, out):
+    nc = tc.nc
+    with ExitStack() as ctx:
+        keep = ctx.enter_context(tc.tile_pool(name="keep", bufs=1))
+        psum_s = ctx.enter_context(tc.psum_pool(name="psum_s", bufs=4))
+        psum_t = ctx.enter_context(tc.psum_pool(name="psum_t", bufs=4))
+
+        def cast(engine, dst, src):
+            if engine == "S":
+                nc.scalar.activation(dst, src, ACT.Copy)
+            else:
+                nc.vector.tensor_copy(dst, src)
+
+        offsets = keep.tile([P, N // 16], U16, name="offsets")
+        nc.sync.dma_start(offsets[:], offs)
+        halves = [offsets[:, 32 * h : 32 * h + 32] for h in range(2)]
+
+        dummy = keep.tile([P, 1], F32, name="dummy")
+        nc.gpsimd.memset(dummy[:], 0.0)
+        dummy2 = keep.tile([P, 1], F32, name="dummy2")
+        nc.scalar.activation(dummy2[:], dummy[:], ACT.Exp)
+        ident = keep.tile([P, P], F32, name="ident")
+        make_identity(nc, ident[:])
+
+        q_raw = keep.tile([P, 4, NQ], F32, name="q_raw")
+        k_rows = kT.rearrange("(p j) w -> p j w", j=4)
+        v_rows = vT.rearrange("(p j) w -> p j w", j=2)
+        vs_raw = keep.tile([P, T], F32, name="vs_raw")
+        og_raw = keep.tile([P, QT, DV], F32, name="og_raw")
+        k_chunks = {
+            0: ((0, 512, "S"), (512, 512, "V"), (1024, 512, "S"), (1536, 512, "V")),
+            1: ((0, 512, "S"), (512, 512, "V"), (1024, 512, "S"), (1536, 256, "S"), (1792, 256, "V")),
+        }
+        k_raw = {}
+        v_raw = {}
+
+        def load_k(u):
+            for c0, cw, _ in k_chunks[u]:
+                t = keep.tile([P, 2, cw], F32, name=f"k_raw{u}_{c0}")
+                nc.sync.dma_start(t[:], k_rows[:, 2 * u : 2 * u + 2, c0 : c0 + cw])
+                k_raw[u, c0] = t
+
+        def load_v(c0, cw):
+            t = keep.tile([P, 2, cw], F32, name=f"v_raw{c0}")
+            nc.sync.dma_start(t[:], v_rows[:, :, c0 : c0 + cw])
+            v_raw[c0] = t
+
+        load_k(0)
+        load_k(1)
+        nc.sync.dma_start(q_raw[:], qT[0].rearrange("(p j) w -> p j w", j=4))
+        load_v(0, 1024)
+        nc.sync.dma_start(vs_raw[:], vs)
+        load_v(1024, 1024)
+        nc.sync.dma_start(og_raw[:], og[0].rearrange("(a p) e -> p a e", p=P))
+
+        k_pair = []
+        k_win = []
+        for u in range(2):
+            t = keep.tile([P, T, 2], BF16, name=f"k_pair{u}")
+            k_pair.append(t)
+            k_win.append(t[:].rearrange("p w j -> p (w j)").bitcast(U32))
+        k_gath = []
+        k_codes = []
+        k_scales = []
+        for h in range(2):
+            k_gath.append(keep.tile([P, HALF, 4], BF16, name=f"k_gath{h}", align_bytes=64))
+            k_codes.append(keep.tile([P, HALF], U32, name=f"k_codes{h}", align_bytes=64))
+            k_scales.append(keep.tile([P, HALF], U8, name=f"k_scales{h}", align_bytes=64))
+
+        def cast_k(u):
+            for c0, cw, e in k_chunks[u]:
+                cast(e, k_pair[u][:, c0 : c0 + cw, :], k_raw[u, c0][:].rearrange("p j w -> p w j"))
+
+        def gather_k(u, h):
+            words = k_gath[h][:].rearrange("p n j -> p (n j)").bitcast(U32)
+            dst = words.rearrange("p (t s u) -> p s t u", t=4, u=2)[:, :, :, u]
+            nc.vector.tensor_copy(dst, k_win[u].indirect(halves[h]))
+
+        def quantize(codes, scales, bf):
+            nc.vector.quantize_mx(out=codes.bitcast(FP8X4), scales=scales, in_=bf.rearrange("p n j -> p (n j)"))
+
+        q_bf = keep.tile([P, NQ, 4], BF16, name="q_bf", align_bytes=64)
+        q_codes = keep.tile([P, NQ], U32, name="q_codes", align_bytes=64)
+        q_scales = keep.tile([P, NQ], U8, name="q_scales", align_bytes=64)
+
+        def do_q():
+            cast("S", q_bf[:], q_raw[:].rearrange("p j w -> p w j"))
+            quantize(q_codes[:], q_scales[:], q_bf[:])
+
+        th = {}
+        nmx = {}
+        for a in range(QT):
+            th[a] = keep.tile([P, 2, HALF], F32, name=f"th{a}")
+
+        def scores(h):
+            for a in range(QT):
+                s_ps = psum_s.tile([P, HALF], F32, name="s_ps")
+                qs = slice(a * P, (a + 1) * P)
+                nc.tensor.matmul_mx(
+                    out=s_ps[:],
+                    lhsT=q_codes[:, qs].bitcast(FP8X4),
+                    lhsT_scale=q_scales[:, qs],
+                    rhs=k_codes[h][:].bitcast(FP8X4),
+                    rhs_scale=k_scales[h][:],
+                    start=True,
+                    stop=True,
+                )
+                nc.scalar.activation(th[a][:, h, :], s_ps[:], ACT.Tanh, scale=0.5)
+
+        def row_max(a, h):
+            m = keep.tile([P, 1], F32, name=f"nmx{a}{h}")
+            nc.vector.tensor_reduce(m[:], th[a][:, h, :], AX.X, ALU.max, negate=True)
+            nmx[a, h] = m
+
+        vs_g = []
+        vs_t = []
+
+        def gather_vs(h):
+            g = keep.tile([P, HALF], F32, name=f"vs_g{h}")
+            nc.vector.tensor_copy(g[:], vs_raw[:].indirect(halves[h]))
+            tp = psum_t.tile([P, 4, P], F32, name="tp")
+            for t in range(4):
+                nc.tensor.transpose(tp[:, t, :], g[:, t:HALF:4], ident[:])
+            s = keep.tile([P, 4], F32, name=f"vs_t{h}")
+            nc.vector.tensor_copy(s[:], tp[:, :, 0])
+            vs_t.append(s)
+
+        v_pair = keep.tile([P, T, 2], BF16, name="v_pair")
+        v_win = v_pair[:].rearrange("p w j -> p (w j)").bitcast(U32)
+
+        def cast_v(chunks):
+            for c0, cw, e in chunks:
+                base = max(b for b in v_raw if b <= c0)
+                src = v_raw[base][:, :, c0 - base : c0 - base + cw]
+                cast(e, v_pair[:, c0 : c0 + cw, :], src.rearrange("p j w -> p w j"))
+
+        v_codes = []
+        v_scales = []
+
+        def do_v(h):
+            v_g = keep.tile([P, HALF], U32, name=f"v_g{h}")
+            nc.vector.tensor_copy(v_g[:], v_win.indirect(halves[h]))
+            tp = psum_t.tile([P, 4, P], F32, name="tp")
+            v_words = v_g[:].bitcast(F32)
+            for t in range(4):
+                nc.tensor.transpose(tp[:, t, :], v_words[:, t:HALF:4], ident[:])
+            v_bf = keep.tile([P, DV, 4], BF16, name=f"v_bf{h}", align_bytes=64)
+            src = tp[:].rearrange("p t w -> p (t w)").bitcast(BF16).rearrange("p (t e) -> p e t", t=4)
+            nc.scalar.copy(v_bf[:], src)
+            c = keep.tile([P, DV], U32, name=f"v_codes{h}", align_bytes=64)
+            s = keep.tile([P, DV], U8, name=f"v_scales{h}", align_bytes=64)
+            quantize(c[:], s[:], v_bf[:])
+            v_codes.append(c)
+            v_scales.append(s)
+
+        neg_m = []
+
+        def finish_max(a):
+            nm = keep.tile([P, 1], F32, name=f"neg_m{a}")
+            nc.vector.tensor_scalar(nm[:], nmx[a, 0][:], nmx[a, 1][:], 2.0, ALU.min, ALU.mult)
+            neg_m.append(nm)
+
+        w_codes = {}
+        w_scales = {}
+        sums = {}
+        p_t = {}
+
+        def weights_exp(a, h):
+            p = keep.tile([P, HALF], F32, name=f"p{a}{h}")
+            l_t = keep.tile([P, 1], F32, name=f"l{a}{h}")
+            nc.scalar.activation(p[:], th[a][:, h, :], ACT.Exp, bias=neg_m[a][:], scale=2.0, accum_out=l_t[:])
+            sums[a, h] = l_t
+            p_t[a, h] = p
+
+        def weights_turn(a, h):
+            tp = psum_t.tile([P, 4, P], F32, name="tp")
+            for t in range(4):
+                nc.tensor.transpose(tp[:, t, :], p_t[a, h][:, t * P : (t + 1) * P], ident[:])
+            w_bf = keep.tile([P, P, 4], BF16, name=f"w_bf{a}{h}", align_bytes=64)
+            nc.vector.tensor_tensor(
+                w_bf[:],
+                tp[:].rearrange("p t q -> p q t"),
+                vs_t[h][:].unsqueeze(1).to_broadcast([P, P, 4]),
+                ALU.mult,
+            )
+            c = keep.tile([P, P], U32, name=f"w_codes{a}{h}", align_bytes=64)
+            s = keep.tile([P, P], U8, name=f"w_scales{a}{h}", align_bytes=64)
+            quantize(c[:], s[:], w_bf[:])
+            w_codes[a, h] = c
+            w_scales[a, h] = s
+
+        gate = keep.tile([P, QT, DV], F32, name="gate")
+
+        def do_gate():
+            g = keep.tile([P, QT, DV], F32, name="gate_t")
+            nc.scalar.activation(g[:], og_raw[:], ACT.Tanh, scale=0.5)
+            nc.gpsimd.tensor_scalar(gate[:], g[:], 0.5, 0.5, ALU.mult, ALU.add)
+
+        def finish(a):
+            l_sum = keep.tile([P, 1], F32, name=f"l_sum{a}")
+            nc.vector.tensor_tensor(l_sum[:], sums[a, 0][:], sums[a, 1][:], ALU.add)
+            r_l = keep.tile([P, 1], F32, name=f"r_l{a}")
+            nc.vector.reciprocal(r_l[:], l_sum[:])
+            y_ps = psum_s.tile([P, HALF], F32, name="s_ps")
+            for h in range(2):
+                nc.tensor.matmul_mx(
+                    out=y_ps[:, 0:DV],
+                    lhsT=w_codes[a, h][:].bitcast(FP8X4),
+                    lhsT_scale=w_scales[a, h][:],
+                    rhs=v_codes[h][:].bitcast(FP8X4),
+                    rhs_scale=v_scales[h][:],
+                    start=(h == 0),
+                    stop=(h == 1),
+                )
+            o = keep.tile([P, DV], F32, name=f"o{a}")
+            nc.vector.scalar_tensor_tensor(o[:], y_ps[:, 0:DV], r_l[:], gate[:, a, :], ALU.mult, ALU.mult)
+            nc.sync.dma_start(out[0, a * P : (a + 1) * P, :], o[:])
+
+        cast_k(0)
+        gather_k(0, 0)
+        gather_k(0, 1)
+        cast_k(1)
+        gather_k(1, 0)
+        do_q()
+        quantize(k_codes[0][:], k_scales[0][:], k_gath[0][:])
+        gather_k(1, 1)
+        quantize(k_codes[1][:], k_scales[1][:], k_gath[1][:])
+        scores(0)
+        scores(1)
+        for h in range(2):
+            for a in range(QT):
+                row_max(a, h)
+        for a in range(QT):
+            finish_max(a)
+        gather_vs(0)
+        gather_vs(1)
+        for a in range(QT):
+            for h in range(2):
+                weights_exp(a, h)
+                weights_turn(a, h)
+        cast_v(((0, 512, "S"), (512, 512, "S"), (1024, 512, "S"), (1536, 512, "S")))
+        do_gate()
+        do_v(0)
+        do_v(1)
+        for a in range(QT):
+            finish(a)

@@ -24,8 +24,11 @@ def tile_attend_x_cap_gate_topk_kernel(tc, qT, kT, vT, vs, og, offs, out):
     nc = tc.nc
     with ExitStack() as ctx:
         keep = ctx.enter_context(tc.tile_pool(name="keep", bufs=1))
-        psum_s = ctx.enter_context(tc.psum_pool(name="psum_s", bufs=4))
-        psum_t = ctx.enter_context(tc.psum_pool(name="psum_t", bufs=4))
+        ring = ctx.enter_context(tc.tile_pool(name="ring", bufs=5))
+        turn = ctx.enter_context(tc.tile_pool(name="turn", bufs=1))
+        psum_s = ctx.enter_context(tc.psum_pool(name="psum_s", bufs=3))
+        psum_t = ctx.enter_context(tc.psum_pool(name="psum_t", bufs=3))
+        psum_v = ctx.enter_context(tc.psum_pool(name="psum_v", bufs=2))
 
         def cast(engine, dst, src):
             if engine == "S":
@@ -44,36 +47,28 @@ def tile_attend_x_cap_gate_topk_kernel(tc, qT, kT, vT, vs, og, offs, out):
         ident = keep.tile([P, P], F32, name="ident")
         make_identity(nc, ident[:])
 
-        q_raw = keep.tile([P, 4, NQ], F32, name="q_raw")
         k_rows = kT.rearrange("(p j) w -> p j w", j=4)
         v_rows = vT.rearrange("(p j) w -> p j w", j=2)
-        vs_raw = keep.tile([P, T], F32, name="vs_raw")
+        shared = {}
         og_raw = keep.tile([P, QT, DV], F32, name="og_raw")
-        k_chunks = {
-            0: ((0, 512, "S"), (512, 512, "V"), (1024, 512, "S"), (1536, 512, "V")),
-            1: ((0, 512, "S"), (512, 512, "V"), (1024, 512, "S"), (1536, 256, "S"), (1792, 256, "V")),
-        }
-        k_raw = {}
-        v_raw = {}
+        chunks = [(u, c0) for u in range(3) for c0 in range(0, T, 512)]
+        engines = "SSSVSSSVSSSV"
+        raw = {}
 
-        def load_k(u):
-            for c0, cw, _ in k_chunks[u]:
-                t = keep.tile([P, 2, cw], F32, name=f"k_raw{u}_{c0}")
-                nc.sync.dma_start(t[:], k_rows[:, 2 * u : 2 * u + 2, c0 : c0 + cw])
-                k_raw[u, c0] = t
+        def load(i):
+            u, c0 = chunks[i]
+            rows = v_rows if u == 2 else k_rows[:, 2 * u : 2 * u + 2]
+            t = ring.tile([P, 2, 512], F32, name="raw")
+            nc.sync.dma_start(t[:], rows[:, :, c0 : c0 + 512])
+            raw[i] = t
 
-        def load_v(c0, cw):
-            t = keep.tile([P, 2, cw], F32, name=f"v_raw{c0}")
-            nc.sync.dma_start(t[:], v_rows[:, :, c0 : c0 + cw])
-            v_raw[c0] = t
+        v_pair = keep.tile([P, T, 2], BF16, name="v_pair")
+        v_win = v_pair[:].rearrange("p w j -> p (w j)").bitcast(U32)
 
-        load_k(0)
-        load_k(1)
-        nc.sync.dma_start(q_raw[:], qT[0].rearrange("(p j) w -> p j w", j=4))
-        load_v(0, 1024)
-        nc.sync.dma_start(vs_raw[:], vs)
-        load_v(1024, 1024)
-        nc.sync.dma_start(og_raw[:], og[0].rearrange("(a p) e -> p a e", p=P))
+        def cast_chunk(i):
+            u, c0 = chunks[i]
+            pair = v_pair if u == 2 else k_pair[u]
+            cast(engines[i], pair[:, c0 : c0 + 512, :], raw[i][:].rearrange("p j w -> p w j"))
 
         k_pair = []
         k_win = []
@@ -89,10 +84,6 @@ def tile_attend_x_cap_gate_topk_kernel(tc, qT, kT, vT, vs, og, offs, out):
             k_codes.append(keep.tile([P, HALF], U32, name=f"k_codes{h}", align_bytes=64))
             k_scales.append(keep.tile([P, HALF], U8, name=f"k_scales{h}", align_bytes=64))
 
-        def cast_k(u):
-            for c0, cw, e in k_chunks[u]:
-                cast(e, k_pair[u][:, c0 : c0 + cw, :], k_raw[u, c0][:].rearrange("p j w -> p w j"))
-
         def gather_k(u, h):
             words = k_gath[h][:].rearrange("p n j -> p (n j)").bitcast(U32)
             dst = words.rearrange("p (t s u) -> p s t u", t=4, u=2)[:, :, :, u]
@@ -105,82 +96,98 @@ def tile_attend_x_cap_gate_topk_kernel(tc, qT, kT, vT, vs, og, offs, out):
         q_codes = keep.tile([P, NQ], U32, name="q_codes", align_bytes=64)
         q_scales = keep.tile([P, NQ], U8, name="q_scales", align_bytes=64)
 
-        def do_q():
-            cast("S", q_bf[:], q_raw[:].rearrange("p j w -> p w j"))
-            quantize(q_codes[:], q_scales[:], q_bf[:])
+        def load_q():
+            shared["q"] = turn.tile([P, 4, NQ], F32, name="q_raw", tag="turn")
+            nc.sync.dma_start(shared["q"][:], qT[0].rearrange("(p j) w -> p j w", j=4))
+
+        def load_vs():
+            shared["vs"] = turn.tile([P, T], F32, name="vs_raw", tag="turn")
+            nc.sync.dma_start(shared["vs"][:], vs)
+
+        def load_og():
+            nc.sync.dma_start(og_raw[:], og[0].rearrange("(a p) e -> p a e", p=P))
+
+        def cast_q():
+            cast("S", q_bf[:], shared["q"][:].rearrange("p j w -> p w j"))
 
         th = {}
         nmx = {}
         for a in range(QT):
             th[a] = keep.tile([P, 2, HALF], F32, name=f"th{a}")
 
-        def scores(h):
-            for a in range(QT):
-                s_ps = psum_s.tile([P, HALF], F32, name="s_ps")
-                qs = slice(a * P, (a + 1) * P)
-                nc.tensor.matmul_mx(
-                    out=s_ps[:],
-                    lhsT=q_codes[:, qs].bitcast(FP8X4),
-                    lhsT_scale=q_scales[:, qs],
-                    rhs=k_codes[h][:].bitcast(FP8X4),
-                    rhs_scale=k_scales[h][:],
-                    start=True,
-                    stop=True,
-                )
-                nc.scalar.activation(th[a][:, h, :], s_ps[:], ACT.Tanh, scale=0.5)
+        def score(a, h):
+            s_ps = psum_s.tile([P, HALF], F32, name="s_ps")
+            qs = slice(a * P, (a + 1) * P)
+            nc.tensor.matmul_mx(
+                out=s_ps[:],
+                lhsT=q_codes[:, qs].bitcast(FP8X4),
+                lhsT_scale=q_scales[:, qs],
+                rhs=k_codes[h][:].bitcast(FP8X4),
+                rhs_scale=k_scales[h][:],
+                start=True,
+                stop=True,
+            )
+            nc.scalar.activation(th[a][:, h, :], s_ps[:], ACT.Tanh, scale=0.5)
 
         def row_max(a, h):
             m = keep.tile([P, 1], F32, name=f"nmx{a}{h}")
             nc.vector.tensor_reduce(m[:], th[a][:, h, :], AX.X, ALU.max, negate=True)
             nmx[a, h] = m
 
-        vs_g = []
-        vs_t = []
+        vs_g = {}
+        vs_t = {}
+
+        vs_tp = {}
 
         def gather_vs(h):
             g = keep.tile([P, HALF], F32, name=f"vs_g{h}")
-            nc.vector.tensor_copy(g[:], vs_raw[:].indirect(halves[h]))
-            tp = psum_t.tile([P, 4, P], F32, name="tp")
+            nc.vector.tensor_copy(g[:], shared["vs"][:].indirect(halves[h]))
+            vs_g[h] = g
+
+        def turn_vs(h):
+            vs_tp[h] = psum_v.tile([P, 4, P], F32, name="tv")
             for t in range(4):
-                nc.tensor.transpose(tp[:, t, :], g[:, t:HALF:4], ident[:])
-            s = keep.tile([P, 4], F32, name=f"vs_t{h}")
-            nc.vector.tensor_copy(s[:], tp[:, :, 0])
-            vs_t.append(s)
+                nc.tensor.transpose(vs_tp[h][:, t, :], vs_g[h][:, t:HALF:4], ident[:])
 
-        v_pair = keep.tile([P, T, 2], BF16, name="v_pair")
-        v_win = v_pair[:].rearrange("p w j -> p (w j)").bitcast(U32)
+        def column_vs(h):
+            vs_t[h] = keep.tile([P, 4], F32, name=f"vs_t{h}")
+            nc.vector.tensor_copy(vs_t[h][:], vs_tp[h][:, :, 0])
 
-        def cast_v(chunks):
-            for c0, cw, e in chunks:
-                base = max(b for b in v_raw if b <= c0)
-                src = v_raw[base][:, :, c0 - base : c0 - base + cw]
-                cast(e, v_pair[:, c0 : c0 + cw, :], src.rearrange("p j w -> p w j"))
+        v_codes = {}
+        v_scales = {}
 
-        v_codes = []
-        v_scales = []
+        v_g = {}
+        v_tp = {}
+        v_bf = {}
 
-        def do_v(h):
-            v_g = keep.tile([P, HALF], U32, name=f"v_g{h}")
-            nc.vector.tensor_copy(v_g[:], v_win.indirect(halves[h]))
-            tp = psum_t.tile([P, 4, P], F32, name="tp")
-            v_words = v_g[:].bitcast(F32)
+        def gather_v(h):
+            v_g[h] = keep.tile([P, HALF], U32, name=f"v_g{h}")
+            nc.vector.tensor_copy(v_g[h][:], v_win.indirect(halves[h]))
+
+        def turn_v(h):
+            v_tp[h] = psum_v.tile([P, 4, P], F32, name="tv")
+            v_words = v_g[h][:].bitcast(F32)
             for t in range(4):
-                nc.tensor.transpose(tp[:, t, :], v_words[:, t:HALF:4], ident[:])
-            v_bf = keep.tile([P, DV, 4], BF16, name=f"v_bf{h}", align_bytes=64)
-            src = tp[:].rearrange("p t w -> p (t w)").bitcast(BF16).rearrange("p (t e) -> p e t", t=4)
-            nc.scalar.copy(v_bf[:], src)
+                nc.tensor.transpose(v_tp[h][:, t, :], v_words[:, t:HALF:4], ident[:])
+
+        def evac_v(h):
+            v_bf[h] = keep.tile([P, DV, 4], BF16, name=f"v_bf{h}", align_bytes=64)
+            src = v_tp[h][:].rearrange("p t w -> p (t w)").bitcast(BF16).rearrange("p (t e) -> p e t", t=4)
+            nc.scalar.copy(v_bf[h][:], src)
+
+        def quant_v(h):
             c = keep.tile([P, DV], U32, name=f"v_codes{h}", align_bytes=64)
             s = keep.tile([P, DV], U8, name=f"v_scales{h}", align_bytes=64)
-            quantize(c[:], s[:], v_bf[:])
-            v_codes.append(c)
-            v_scales.append(s)
+            quantize(c[:], s[:], v_bf[h][:])
+            v_codes[h] = c
+            v_scales[h] = s
 
-        neg_m = []
+        neg_m = {}
 
         def finish_max(a):
             nm = keep.tile([P, 1], F32, name=f"neg_m{a}")
             nc.vector.tensor_scalar(nm[:], nmx[a, 0][:], nmx[a, 1][:], 2.0, ALU.min, ALU.mult)
-            neg_m.append(nm)
+            neg_m[a] = nm
 
         w_codes = {}
         w_scales = {}
@@ -194,20 +201,27 @@ def tile_attend_x_cap_gate_topk_kernel(tc, qT, kT, vT, vs, og, offs, out):
             sums[a, h] = l_t
             p_t[a, h] = p
 
-        def weights_turn(a, h):
-            tp = psum_t.tile([P, 4, P], F32, name="tp")
+        w_tp = {}
+        w_bf = {}
+
+        def turn_w(a, h):
+            w_tp[a, h] = psum_t.tile([P, 4, P], F32, name="tp")
             for t in range(4):
-                nc.tensor.transpose(tp[:, t, :], p_t[a, h][:, t * P : (t + 1) * P], ident[:])
-            w_bf = keep.tile([P, P, 4], BF16, name=f"w_bf{a}{h}", align_bytes=64)
+                nc.tensor.transpose(w_tp[a, h][:, t, :], p_t[a, h][:, t * P : (t + 1) * P], ident[:])
+
+        def scale_w(a, h):
+            w_bf[a, h] = keep.tile([P, P, 4], BF16, name=f"w_bf{a}{h}", align_bytes=64)
             nc.vector.tensor_tensor(
-                w_bf[:],
-                tp[:].rearrange("p t q -> p q t"),
+                w_bf[a, h][:],
+                w_tp[a, h][:].rearrange("p t q -> p q t"),
                 vs_t[h][:].unsqueeze(1).to_broadcast([P, P, 4]),
                 ALU.mult,
             )
+
+        def quant_w(a, h):
             c = keep.tile([P, P], U32, name=f"w_codes{a}{h}", align_bytes=64)
             s = keep.tile([P, P], U8, name=f"w_scales{a}{h}", align_bytes=64)
-            quantize(c[:], s[:], w_bf[:])
+            quantize(c[:], s[:], w_bf[a, h][:])
             w_codes[a, h] = c
             w_scales[a, h] = s
 
@@ -218,11 +232,16 @@ def tile_attend_x_cap_gate_topk_kernel(tc, qT, kT, vT, vs, og, offs, out):
             nc.scalar.activation(g[:], og_raw[:], ACT.Tanh, scale=0.5)
             nc.gpsimd.tensor_scalar(gate[:], g[:], 0.5, 0.5, ALU.mult, ALU.add)
 
-        def finish(a):
+        r_l = {}
+        y_tp = {}
+
+        def inverse_sum(a):
             l_sum = keep.tile([P, 1], F32, name=f"l_sum{a}")
             nc.vector.tensor_tensor(l_sum[:], sums[a, 0][:], sums[a, 1][:], ALU.add)
-            r_l = keep.tile([P, 1], F32, name=f"r_l{a}")
-            nc.vector.reciprocal(r_l[:], l_sum[:])
+            r_l[a] = keep.tile([P, 1], F32, name=f"r_l{a}")
+            nc.vector.reciprocal(r_l[a][:], l_sum[:])
+
+        def product(a):
             y_ps = psum_s.tile([P, HALF], F32, name="s_ps")
             for h in range(2):
                 nc.tensor.matmul_mx(
@@ -234,35 +253,91 @@ def tile_attend_x_cap_gate_topk_kernel(tc, qT, kT, vT, vs, og, offs, out):
                     start=(h == 0),
                     stop=(h == 1),
                 )
+            y_tp[a] = y_ps
+
+        def finish(a):
+            y_ps = y_tp[a]
             o = keep.tile([P, DV], F32, name=f"o{a}")
-            nc.vector.scalar_tensor_tensor(o[:], y_ps[:, 0:DV], r_l[:], gate[:, a, :], ALU.mult, ALU.mult)
+            nc.vector.scalar_tensor_tensor(o[:], y_ps[:, 0:DV], r_l[a][:], gate[:, a, :], ALU.mult, ALU.mult)
             nc.sync.dma_start(out[0, a * P : (a + 1) * P, :], o[:])
 
-        cast_k(0)
+        for i in range(4):
+            load(i)
+        load_q()
+        load(4)
+        cast_chunk(0)
+        load(5)
+        cast_chunk(1)
+        load(6)
+        cast_chunk(2)
+        load(7)
+        cast_chunk(3)
+        load(8)
         gather_k(0, 0)
+        cast_q()
         gather_k(0, 1)
-        cast_k(1)
+        cast_chunk(4)
+        load(9)
+        load_vs()
+        quantize(q_codes[:], q_scales[:], q_bf[:])
+        cast_chunk(5)
+        load(10)
+        cast_chunk(6)
+        load(11)
+        cast_chunk(7)
+        load_og()
         gather_k(1, 0)
-        do_q()
-        quantize(k_codes[0][:], k_scales[0][:], k_gath[0][:])
+        cast_chunk(8)
         gather_k(1, 1)
+        cast_chunk(9)
+        quantize(k_codes[0][:], k_scales[0][:], k_gath[0][:])
         quantize(k_codes[1][:], k_scales[1][:], k_gath[1][:])
-        scores(0)
-        scores(1)
-        for h in range(2):
-            for a in range(QT):
-                row_max(a, h)
-        for a in range(QT):
-            finish_max(a)
+        score(0, 0)
         gather_vs(0)
+        score(1, 0)
+        score(0, 1)
         gather_vs(1)
-        for a in range(QT):
-            for h in range(2):
-                weights_exp(a, h)
-                weights_turn(a, h)
-        cast_v(((0, 512, "S"), (512, 512, "S"), (1024, 512, "S"), (1536, 512, "S")))
+        score(1, 1)
+        turn_vs(0)
+        row_max(0, 0)
+        turn_vs(1)
+        row_max(0, 1)
         do_gate()
-        do_v(0)
-        do_v(1)
-        for a in range(QT):
-            finish(a)
+        row_max(1, 0)
+        cast_chunk(10)
+        finish_max(0)
+        row_max(1, 1)
+        weights_exp(0, 1)
+        cast_chunk(11)
+        weights_exp(0, 0)
+        finish_max(1)
+        column_vs(1)
+        column_vs(0)
+        gather_v(1)
+        turn_w(0, 1)
+        weights_exp(1, 1)
+        turn_w(0, 0)
+        weights_exp(1, 0)
+        inverse_sum(0)
+        gather_v(0)
+        turn_v(1)
+        turn_w(1, 0)
+        scale_w(0, 0)
+        evac_v(1)
+        turn_v(0)
+        scale_w(0, 1)
+        turn_w(1, 1)
+        quant_w(0, 0)
+        scale_w(1, 0)
+        evac_v(0)
+        quant_v(1)
+        quant_w(0, 1)
+        quant_w(1, 0)
+        scale_w(1, 1)
+        quant_v(0)
+        quant_w(1, 1)
+        inverse_sum(1)
+        product(0)
+        product(1)
+        finish(0)
+        finish(1)

@@ -24,7 +24,6 @@ def tile_attend_x_cap_gate_topk_kernel(tc, qT, kT, vT, vs, og, offs, out):
     nc = tc.nc
     with ExitStack() as ctx:
         keep = ctx.enter_context(tc.tile_pool(name="keep", bufs=1))
-        ring = ctx.enter_context(tc.tile_pool(name="ring", bufs=5))
         turn = ctx.enter_context(tc.tile_pool(name="turn", bufs=1))
         psum_s = ctx.enter_context(tc.psum_pool(name="psum_s", bufs=3))
         psum_t = ctx.enter_context(tc.psum_pool(name="psum_t", bufs=3))
@@ -51,24 +50,26 @@ def tile_attend_x_cap_gate_topk_kernel(tc, qT, kT, vT, vs, og, offs, out):
         v_rows = vT.rearrange("(p j) w -> p j w", j=2)
         shared = {}
         og_raw = keep.tile([P, QT, DV], F32, name="og_raw")
-        chunks = [(u, c0) for u in range(3) for c0 in range(0, T, 512)]
-        engines = "SSSVSSSVSSSV"
         raw = {}
 
-        def load(i):
-            u, c0 = chunks[i]
+        def load(u, i):
             rows = v_rows if u == 2 else k_rows[:, 2 * u : 2 * u + 2]
-            t = ring.tile([P, 2, 512], F32, name="raw")
-            nc.sync.dma_start(t[:], rows[:, :, c0 : c0 + 512])
-            raw[i] = t
+            if (u, i) == (2, 0):
+                raw[u, i] = turn.tile([P, 2, 1024], F32, name="raw20", tag="v0")
+            elif (u, i) == (2, 1):
+                raw[u, i] = turn.tile([P, 2, 1024], F32, name="raw21", tag="v1")
+            else:
+                raw[u, i] = keep.tile([P, 2, 1024], F32, name=f"raw{u}{i}")
+            nc.sync.dma_start(raw[u, i][:], rows[:, :, 1024 * i : 1024 * (i + 1)])
 
         v_pair = keep.tile([P, T, 2], BF16, name="v_pair")
         v_win = v_pair[:].rearrange("p w j -> p (w j)").bitcast(U32)
 
-        def cast_chunk(i):
-            u, c0 = chunks[i]
+        def cast_piece(u, c0, cw, engine):
             pair = v_pair if u == 2 else k_pair[u]
-            cast(engines[i], pair[:, c0 : c0 + 512, :], raw[i][:].rearrange("p j w -> p w j"))
+            i = c0 // 1024
+            src = raw[u, i][:, :, c0 - 1024 * i : c0 - 1024 * i + cw]
+            cast(engine, pair[:, c0 : c0 + cw, :], src.rearrange("p j w -> p w j"))
 
         k_pair = []
         k_win = []
@@ -97,7 +98,7 @@ def tile_attend_x_cap_gate_topk_kernel(tc, qT, kT, vT, vs, og, offs, out):
         q_scales = keep.tile([P, NQ], U8, name="q_scales", align_bytes=64)
 
         def load_q():
-            shared["q"] = turn.tile([P, 4, NQ], F32, name="q_raw", tag="turn")
+            shared["q"] = keep.tile([P, 4, NQ], F32, name="q_raw")
             nc.sync.dma_start(shared["q"][:], qT[0].rearrange("(p j) w -> p j w", j=4))
 
         def load_vs():
@@ -111,9 +112,8 @@ def tile_attend_x_cap_gate_topk_kernel(tc, qT, kT, vT, vs, og, offs, out):
             cast("S", q_bf[:], shared["q"][:].rearrange("p j w -> p w j"))
 
         th = {}
+        s_tp = {}
         nmx = {}
-        for a in range(QT):
-            th[a] = keep.tile([P, 2, HALF], F32, name=f"th{a}")
 
         def score(a, h):
             s_ps = psum_s.tile([P, HALF], F32, name="s_ps")
@@ -127,22 +127,32 @@ def tile_attend_x_cap_gate_topk_kernel(tc, qT, kT, vT, vs, og, offs, out):
                 start=True,
                 stop=True,
             )
-            nc.scalar.activation(th[a][:, h, :], s_ps[:], ACT.Tanh, scale=0.5)
+            s_tp[a, h] = s_ps
+
+        def cap(a, h):
+            if not th:
+                both = turn.tile([P, QT, 2, HALF], F32, name="th", tag="v0")
+                for i in range(QT):
+                    th[i] = both[:, i, :, :]
+            nc.scalar.activation(th[a][:, h, :], s_tp[a, h][:], ACT.Tanh, scale=0.5)
 
         def row_max(a, h):
-            m = keep.tile([P, 1], F32, name=f"nmx{a}{h}")
-            nc.vector.tensor_reduce(m[:], th[a][:, h, :], AX.X, ALU.max, negate=True)
-            nmx[a, h] = m
+            if not nmx:
+                t = turn.tile([P, 2 * QT], F32, name="nmx", tag="turn")
+                for i in range(2 * QT):
+                    nmx[i // 2, i % 2] = t[:, i : i + 1]
+            nc.vector.tensor_reduce(nmx[a, h], th[a][:, h, :], AX.X, ALU.max, negate=True)
 
         vs_g = {}
         vs_t = {}
 
         vs_tp = {}
 
-        def gather_vs(h):
-            g = keep.tile([P, HALF], F32, name=f"vs_g{h}")
-            nc.vector.tensor_copy(g[:], shared["vs"][:].indirect(halves[h]))
-            vs_g[h] = g
+        def gather_vs():
+            g = keep.tile([P, N], F32, name="vs_g")
+            nc.vector.tensor_copy(g[:], shared["vs"][:].indirect(offsets[:]))
+            for h in range(2):
+                vs_g[h] = g[:, h * HALF : (h + 1) * HALF]
 
         def turn_vs(h):
             vs_tp[h] = psum_v.tile([P, 4, P], F32, name="tv")
@@ -186,7 +196,7 @@ def tile_attend_x_cap_gate_topk_kernel(tc, qT, kT, vT, vs, og, offs, out):
 
         def finish_max(a):
             nm = keep.tile([P, 1], F32, name=f"neg_m{a}")
-            nc.vector.tensor_scalar(nm[:], nmx[a, 0][:], nmx[a, 1][:], 2.0, ALU.min, ALU.mult)
+            nc.vector.tensor_scalar(nm[:], nmx[a, 0], nmx[a, 1], 2.0, ALU.min, ALU.mult)
             neg_m[a] = nm
 
         w_codes = {}
@@ -195,11 +205,14 @@ def tile_attend_x_cap_gate_topk_kernel(tc, qT, kT, vT, vs, og, offs, out):
         p_t = {}
 
         def weights_exp(a, h):
-            p = keep.tile([P, HALF], F32, name=f"p{a}{h}")
+            if not p_t:
+                every = turn.tile([P, QT, 2, HALF], F32, name="p", tag="v1")
+                for i in range(2 * QT):
+                    p_t[i // 2, i % 2] = every[:, i // 2, i % 2, :]
+            p = p_t[a, h]
             l_t = keep.tile([P, 1], F32, name=f"l{a}{h}")
-            nc.scalar.activation(p[:], th[a][:, h, :], ACT.Exp, bias=neg_m[a][:], scale=2.0, accum_out=l_t[:])
+            nc.scalar.activation(p, th[a][:, h, :], ACT.Exp, bias=neg_m[a][:], scale=2.0, accum_out=l_t[:])
             sums[a, h] = l_t
-            p_t[a, h] = p
 
         w_tp = {}
         w_bf = {}
@@ -228,7 +241,7 @@ def tile_attend_x_cap_gate_topk_kernel(tc, qT, kT, vT, vs, og, offs, out):
         gate = keep.tile([P, QT, DV], F32, name="gate")
 
         def do_gate():
-            g = keep.tile([P, QT, DV], F32, name="gate_t")
+            g = turn.tile([P, QT, DV], F32, name="gate_t", tag="v0")
             nc.scalar.activation(g[:], og_raw[:], ACT.Tanh, scale=0.5)
             nc.gpsimd.tensor_scalar(gate[:], g[:], 0.5, 0.5, ALU.mult, ALU.add)
 
@@ -261,83 +274,82 @@ def tile_attend_x_cap_gate_topk_kernel(tc, qT, kT, vT, vs, og, offs, out):
             nc.vector.scalar_tensor_tensor(o[:], y_ps[:, 0:DV], r_l[a][:], gate[:, a, :], ALU.mult, ALU.mult)
             nc.sync.dma_start(out[0, a * P : (a + 1) * P, :], o[:])
 
-        for i in range(4):
-            load(i)
+        load(0, 0)
+        load(0, 1)
+        load(1, 0)
+        load(1, 1)
         load_q()
-        load(4)
-        cast_chunk(0)
-        load(5)
-        cast_chunk(1)
-        load(6)
-        cast_chunk(2)
-        load(7)
-        cast_chunk(3)
-        load(8)
-        gather_k(0, 0)
-        cast_q()
-        gather_k(0, 1)
-        cast_chunk(4)
-        load(9)
+        load(2, 0)
         load_vs()
-        quantize(q_codes[:], q_scales[:], q_bf[:])
-        cast_chunk(5)
-        load(10)
-        cast_chunk(6)
-        load(11)
-        cast_chunk(7)
+        load(2, 1)
         load_og()
+        cast_piece(0, 0, 512, "S")
+        cast_piece(0, 512, 512, "S")
+        cast_piece(0, 1024, 512, "S")
+        cast_piece(0, 1536, 512, "V")
+        gather_k(0, 0)
+        gather_k(0, 1)
+        cast_piece(1, 0, 512, "S")
+        cast_piece(1, 512, 512, "V")
+        cast_piece(1, 1024, 384, "S")
+        cast_piece(1, 1408, 640, "V")
         gather_k(1, 0)
-        cast_chunk(8)
         gather_k(1, 1)
-        cast_chunk(9)
         quantize(k_codes[0][:], k_scales[0][:], k_gath[0][:])
+        cast_q()
+        quantize(q_codes[:], q_scales[:], q_bf[:])
         quantize(k_codes[1][:], k_scales[1][:], k_gath[1][:])
+        cast_piece(2, 0, 512, "S")
+        cast_piece(2, 512, 512, "S")
+        gather_vs()
         score(0, 0)
-        gather_vs(0)
+        cap(0, 0)
         score(1, 0)
+        cap(1, 0)
         score(0, 1)
-        gather_vs(1)
+        cap(0, 1)
         score(1, 1)
+        cap(1, 1)
+        cast_piece(2, 1024, 512, "S")
         turn_vs(0)
-        row_max(0, 0)
         turn_vs(1)
+        row_max(0, 0)
         row_max(0, 1)
-        do_gate()
-        row_max(1, 0)
-        cast_chunk(10)
         finish_max(0)
+        row_max(1, 0)
         row_max(1, 1)
-        weights_exp(0, 1)
-        cast_chunk(11)
-        weights_exp(0, 0)
         finish_max(1)
-        column_vs(1)
-        column_vs(0)
-        gather_v(1)
-        turn_w(0, 1)
-        weights_exp(1, 1)
-        turn_w(0, 0)
+        weights_exp(0, 0)
+        weights_exp(0, 1)
         weights_exp(1, 0)
-        inverse_sum(0)
+        weights_exp(1, 1)
+        cast_piece(2, 1536, 512, "S")
+        column_vs(0)
+        column_vs(1)
         gather_v(0)
-        turn_v(1)
-        turn_w(1, 0)
-        scale_w(0, 0)
-        evac_v(1)
         turn_v(0)
-        scale_w(0, 1)
-        turn_w(1, 1)
-        quant_w(0, 0)
-        scale_w(1, 0)
         evac_v(0)
-        quant_v(1)
-        quant_w(0, 1)
-        quant_w(1, 0)
-        scale_w(1, 1)
+        gather_v(1)
+        turn_v(1)
+        evac_v(1)
         quant_v(0)
+        quant_v(1)
+        turn_w(0, 0)
+        turn_w(0, 1)
+        scale_w(0, 0)
+        scale_w(0, 1)
+        quant_w(0, 0)
+        quant_w(0, 1)
+        turn_w(1, 0)
+        scale_w(1, 0)
+        quant_w(1, 0)
+        turn_w(1, 1)
+        scale_w(1, 1)
         quant_w(1, 1)
-        inverse_sum(1)
         product(0)
         product(1)
+        do_gate()
+        inverse_sum(0)
+        inverse_sum(1)
         finish(0)
         finish(1)

@@ -172,13 +172,14 @@ def tile_attend_x_cap_gate_topk_kernel(tc, qT, kT, vT, vs, og, offs, out):
 
         def gather_v(h):
             v_g[h] = keep.tile([P, HALF], U32, name=f"v_g{h}")
-            nc.vector.tensor_copy(v_g[h][:], v_win.indirect(halves[h]))
+            dst = v_g[h][:].rearrange("p (t s) -> p s t", t=4)
+            nc.vector.tensor_copy(dst, v_win.indirect(halves[h]))
 
         def turn_v(h):
             v_tp[h] = psum_v.tile([P, 4, P], F32, name="tv")
             v_words = v_g[h][:].bitcast(F32)
             for t in range(4):
-                nc.tensor.transpose(v_tp[h][:, t, :], v_words[:, t:HALF:4], ident[:])
+                nc.tensor.transpose(v_tp[h][:, t, :], v_words[:, t * P : (t + 1) * P], ident[:])
 
         def evac_v(h):
             v_bf[h] = keep.tile([P, DV, 4], BF16, name=f"v_bf{h}", align_bytes=64)
@@ -238,21 +239,27 @@ def tile_attend_x_cap_gate_topk_kernel(tc, qT, kT, vT, vs, og, offs, out):
             w_codes[a, h] = c
             w_scales[a, h] = s
 
-        gate = keep.tile([P, QT, DV], F32, name="gate")
+        gate_t = {}
+        gate = {}
 
         def do_gate():
             g = turn.tile([P, QT, DV], F32, name="gate_t", tag="v0")
             nc.scalar.activation(g[:], og_raw[:], ACT.Tanh, scale=0.5)
-            nc.gpsimd.tensor_scalar(gate[:], g[:], 0.5, 0.5, ALU.mult, ALU.add)
+            for a in range(QT):
+                gate_t[a] = g[:, a, :]
 
         r_l = {}
         y_tp = {}
 
         def inverse_sum(a):
             l_sum = keep.tile([P, 1], F32, name=f"l_sum{a}")
-            nc.vector.tensor_tensor(l_sum[:], sums[a, 0][:], sums[a, 1][:], ALU.add)
+            nc.vector.tensor_scalar(l_sum[:], sums[a, 0][:], sums[a, 1][:], 2.0, ALU.add, ALU.mult)
             r_l[a] = keep.tile([P, 1], F32, name=f"r_l{a}")
             nc.vector.reciprocal(r_l[a][:], l_sum[:])
+
+        def scale_gate(a):
+            gate[a] = keep.tile([P, DV], F32, name=f"gate{a}")
+            nc.scalar.activation(gate[a][:], gate_t[a], ACT.Identity, bias=r_l[a][:], scale=r_l[a][:])
 
         def product(a):
             y_ps = psum_s.tile([P, HALF], F32, name="s_ps")
@@ -271,7 +278,7 @@ def tile_attend_x_cap_gate_topk_kernel(tc, qT, kT, vT, vs, og, offs, out):
         def finish(a):
             y_ps = y_tp[a]
             o = keep.tile([P, DV], F32, name=f"o{a}")
-            nc.vector.scalar_tensor_tensor(o[:], y_ps[:, 0:DV], r_l[a][:], gate[:, a, :], ALU.mult, ALU.mult)
+            nc.vector.tensor_tensor(o[:], y_ps[:, 0:DV], gate[a][:], ALU.mult)
             nc.sync.dma_start(out[0, a * P : (a + 1) * P, :], o[:])
 
         load(0, 0)
@@ -310,7 +317,8 @@ def tile_attend_x_cap_gate_topk_kernel(tc, qT, kT, vT, vs, og, offs, out):
         cap(0, 1)
         score(1, 1)
         cap(1, 1)
-        cast_piece(2, 1024, 512, "S")
+        cast_piece(2, 1024, 640, "S")
+        cast_piece(2, 1664, 384, "V")
         turn_vs(0)
         turn_vs(1)
         row_max(0, 0)
@@ -323,7 +331,6 @@ def tile_attend_x_cap_gate_topk_kernel(tc, qT, kT, vT, vs, og, offs, out):
         weights_exp(0, 1)
         weights_exp(1, 0)
         weights_exp(1, 1)
-        cast_piece(2, 1536, 512, "S")
         column_vs(0)
         column_vs(1)
         gather_v(0)
@@ -350,6 +357,8 @@ def tile_attend_x_cap_gate_topk_kernel(tc, qT, kT, vT, vs, og, offs, out):
         product(1)
         do_gate()
         inverse_sum(0)
+        scale_gate(0)
         inverse_sum(1)
+        scale_gate(1)
         finish(0)
         finish(1)

@@ -5,7 +5,9 @@ from concourse.masks import make_identity
 
 P = 128
 NQ, D, DV, T, N = 256, 512, 256, 2048, 1024
-HALF = 512
+PACK = 4
+PASS = P * PACK
+HALVES = N // PASS
 QT = NQ // P
 FLOPS = 2 * NQ * N * (D + DV)
 
@@ -19,346 +21,305 @@ ACT = mybir.ActivationFunctionType
 ALU = mybir.AluOpType
 AX = mybir.AxisListType
 
+KEYS_LOW, KEYS_HIGH, VALUES = 0, 1, 2
+KEY_LOADS = (
+    (KEYS_LOW, 0, 1024),
+    (KEYS_LOW, 1024, 1024),
+    (KEYS_HIGH, 0, 1024),
+    (KEYS_HIGH, 1024, 768),
+    (KEYS_HIGH, 1792, 256),
+)
+CASTS = {
+    KEYS_LOW: ((0, 512, True), (512, 512, True), (1024, 448, True), (1472, 576, False)),
+    KEYS_HIGH: (
+        (0, 512, True),
+        (512, 512, True),
+        (1024, 320, True),
+        (1344, 448, False),
+        (1792, 256, False),
+    ),
+    VALUES: ((0, 512, True), (512, 512, True), (1024, 640, True), (1664, 384, False)),
+}
+
 
 def tile_attend_x_cap_gate_topk_kernel(tc, qT, kT, vT, vs, og, offs, out):
     nc = tc.nc
     with ExitStack() as ctx:
         keep = ctx.enter_context(tc.tile_pool(name="keep", bufs=1))
-        turn = ctx.enter_context(tc.tile_pool(name="turn", bufs=1))
-        psum_s = ctx.enter_context(tc.psum_pool(name="psum_s", bufs=3))
-        psum_t = ctx.enter_context(tc.psum_pool(name="psum_t", bufs=3))
-        psum_v = ctx.enter_context(tc.psum_pool(name="psum_v", bufs=2))
+        handover = ctx.enter_context(tc.tile_pool(name="handover", bufs=1))
+        psum_scores = ctx.enter_context(tc.psum_pool(name="psum_scores", bufs=3))
+        psum_weights = ctx.enter_context(tc.psum_pool(name="psum_weights", bufs=3))
+        psum_slots = ctx.enter_context(tc.psum_pool(name="psum_slots", bufs=2))
 
-        def cast(engine, dst, src):
-            if engine == "S":
+        half = keep.tile([P, 1], F32, name="half")
+        nc.gpsimd.memset(half[:], 0.5)
+        warm = keep.tile([P, 1], F32, name="warm")
+        nc.scalar.activation(warm[:], half[:], ACT.Exp)
+        ident = keep.tile([P, P], F32, name="ident")
+        make_identity(nc, ident[:])
+
+        k_rows = kT.rearrange("(p j) w -> p j w", j=PACK)
+        v_rows = vT.rearrange("(p j) w -> p j w", j=2)
+        raw = {}
+
+        def load(pair, c0, cw, tag=None):
+            rows = v_rows if pair == VALUES else k_rows[:, 2 * pair : 2 * pair + 2, :]
+            name = f"raw{pair}_{c0}"
+            if tag is None:
+                tile = keep.tile([P, 2, cw], F32, name=name)
+            else:
+                tile = handover.tile([P, 2, cw], F32, name=name, tag=tag)
+            nc.sync.dma_start(tile[:], rows[:, :, c0 : c0 + cw])
+            raw[pair, c0] = tile
+
+        offsets = keep.tile([P, N // 16], U16, name="offsets")
+        load(*KEY_LOADS[0])
+        nc.sync.dma_start(offsets[:], offs)
+        for each in KEY_LOADS[1:]:
+            load(*each)
+        q_raw = keep.tile([P, PACK, NQ], F32, name="q_raw")
+        nc.sync.dma_start(q_raw[:], qT[0].rearrange("(p j) w -> p j w", j=PACK))
+        load(VALUES, 0, T // 2, tag="values0")
+        vs_raw = handover.tile([P, T], F32, name="vs_raw", tag="scales")
+        nc.sync.dma_start(vs_raw[:], vs)
+        load(VALUES, T // 2, T // 2, tag="values1")
+        og_raw = keep.tile([P, QT, DV], F32, name="og_raw")
+        nc.sync.dma_start(og_raw[:], og[0].rearrange("(a p) e -> p a e", p=P))
+
+        columns = PASS // 16
+        slots = [offsets[:, h * columns : (h + 1) * columns] for h in range(HALVES)]
+
+        paired = []
+        window = []
+        for pair in (KEYS_LOW, KEYS_HIGH, VALUES):
+            tile = keep.tile([P, T, 2], BF16, name=f"paired{pair}")
+            paired.append(tile)
+            window.append(tile[:].rearrange("p w j -> p (w j)").bitcast(U32))
+
+        def cast(pair, c0, cw, on_scalar):
+            start = max(s for owner, s in raw if owner == pair and s <= c0)
+            src = raw[pair, start][:, :, c0 - start : c0 - start + cw].rearrange("p j w -> p w j")
+            dst = paired[pair][:, c0 : c0 + cw, :]
+            if on_scalar:
                 nc.scalar.activation(dst, src, ACT.Copy)
             else:
                 nc.vector.tensor_copy(dst, src)
 
-        offsets = keep.tile([P, N // 16], U16, name="offsets")
-        nc.sync.dma_start(offsets[:], offs)
-        halves = [offsets[:, 32 * h : 32 * h + 32] for h in range(2)]
+        def quantize(codes, scales, grouped):
+            nc.vector.quantize_mx(
+                out=codes.bitcast(FP8X4), scales=scales, in_=grouped.rearrange("p n t -> p (n t)")
+            )
 
-        dummy = keep.tile([P, 1], F32, name="dummy")
-        nc.gpsimd.memset(dummy[:], 0.0)
-        dummy2 = keep.tile([P, 1], F32, name="dummy2")
-        nc.scalar.activation(dummy2[:], dummy[:], ACT.Exp)
-        ident = keep.tile([P, P], F32, name="ident")
-        make_identity(nc, ident[:])
+        def packed(width, name):
+            codes = keep.tile([P, width], U32, name=f"{name}_codes", align_bytes=64)
+            scales = keep.tile([P, width], U8, name=f"{name}_scales", align_bytes=64)
+            return codes, scales
 
-        k_rows = kT.rearrange("(p j) w -> p j w", j=4)
-        v_rows = vT.rearrange("(p j) w -> p j w", j=2)
-        shared = {}
-        og_raw = keep.tile([P, QT, DV], F32, name="og_raw")
-        raw = {}
+        k_grouped = []
+        for h in range(HALVES):
+            k_grouped.append(keep.tile([P, PASS, PACK], BF16, name=f"k_grouped{h}", align_bytes=64))
+        k_packed = [packed(PASS, f"k{h}") for h in range(HALVES)]
 
-        def load(u, i):
-            rows = v_rows if u == 2 else k_rows[:, 2 * u : 2 * u + 2]
-            if (u, i) == (2, 0):
-                raw[u, i] = turn.tile([P, 2, 1024], F32, name="raw20", tag="v0")
-            elif (u, i) == (2, 1):
-                raw[u, i] = turn.tile([P, 2, 1024], F32, name="raw21", tag="v1")
-            else:
-                raw[u, i] = keep.tile([P, 2, 1024], F32, name=f"raw{u}{i}")
-            nc.sync.dma_start(raw[u, i][:], rows[:, :, 1024 * i : 1024 * (i + 1)])
+        def gather_keys(pair, h):
+            words = k_grouped[h][:].rearrange("p n t -> p (n t)").bitcast(U32)
+            by_slot = words.rearrange("p (t s u) -> p s t u", t=PACK, u=2)
+            nc.vector.tensor_copy(by_slot[:, :, :, pair], window[pair].indirect(slots[h]))
 
-        v_pair = keep.tile([P, T, 2], BF16, name="v_pair")
-        v_win = v_pair[:].rearrange("p w j -> p (w j)").bitcast(U32)
+        def quantize_keys(h):
+            quantize(k_packed[h][0][:], k_packed[h][1][:], k_grouped[h][:])
 
-        def cast_piece(u, c0, cw, engine):
-            pair = v_pair if u == 2 else k_pair[u]
-            i = c0 // 1024
-            src = raw[u, i][:, :, c0 - 1024 * i : c0 - 1024 * i + cw]
-            cast(engine, pair[:, c0 : c0 + cw, :], src.rearrange("p j w -> p w j"))
-
-        k_pair = []
-        k_win = []
-        for u in range(2):
-            t = keep.tile([P, T, 2], BF16, name=f"k_pair{u}")
-            k_pair.append(t)
-            k_win.append(t[:].rearrange("p w j -> p (w j)").bitcast(U32))
-        k_gath = []
-        k_codes = []
-        k_scales = []
-        for h in range(2):
-            k_gath.append(keep.tile([P, HALF, 4], BF16, name=f"k_gath{h}", align_bytes=64))
-            k_codes.append(keep.tile([P, HALF], U32, name=f"k_codes{h}", align_bytes=64))
-            k_scales.append(keep.tile([P, HALF], U8, name=f"k_scales{h}", align_bytes=64))
-
-        def gather_k(u, h):
-            words = k_gath[h][:].rearrange("p n j -> p (n j)").bitcast(U32)
-            dst = words.rearrange("p (t s u) -> p s t u", t=4, u=2)[:, :, :, u]
-            nc.vector.tensor_copy(dst, k_win[u].indirect(halves[h]))
-
-        def quantize(codes, scales, bf):
-            nc.vector.quantize_mx(out=codes.bitcast(FP8X4), scales=scales, in_=bf.rearrange("p n j -> p (n j)"))
-
-        q_bf = keep.tile([P, NQ, 4], BF16, name="q_bf", align_bytes=64)
-        q_codes = keep.tile([P, NQ], U32, name="q_codes", align_bytes=64)
-        q_scales = keep.tile([P, NQ], U8, name="q_scales", align_bytes=64)
-
-        def load_q():
-            shared["q"] = keep.tile([P, 4, NQ], F32, name="q_raw")
-            nc.sync.dma_start(shared["q"][:], qT[0].rearrange("(p j) w -> p j w", j=4))
-
-        def load_vs():
-            shared["vs"] = turn.tile([P, T], F32, name="vs_raw", tag="turn")
-            nc.sync.dma_start(shared["vs"][:], vs)
-
-        def load_og():
-            nc.sync.dma_start(og_raw[:], og[0].rearrange("(a p) e -> p a e", p=P))
-
-        def cast_q():
-            cast("S", q_bf[:], shared["q"][:].rearrange("p j w -> p w j"))
-
-        th = {}
-        s_tp = {}
-        nmx = {}
+        score_bank = {}
+        capped = {}
 
         def score(a, h):
-            s_ps = psum_s.tile([P, HALF], F32, name="s_ps")
-            qs = slice(a * P, (a + 1) * P)
+            q_cols = slice(a * P, (a + 1) * P)
+            bank = psum_scores.tile([P, PASS], F32, name="score_bank")
             nc.tensor.matmul_mx(
-                out=s_ps[:],
-                lhsT=q_codes[:, qs].bitcast(FP8X4),
-                lhsT_scale=q_scales[:, qs],
-                rhs=k_codes[h][:].bitcast(FP8X4),
-                rhs_scale=k_scales[h][:],
+                out=bank[:],
+                lhsT=q_packed[0][:, q_cols].bitcast(FP8X4),
+                lhsT_scale=q_packed[1][:, q_cols],
+                rhs=k_packed[h][0][:].bitcast(FP8X4),
+                rhs_scale=k_packed[h][1][:],
                 start=True,
                 stop=True,
             )
-            s_tp[a, h] = s_ps
+            score_bank[a, h] = bank
 
         def cap(a, h):
-            if not th:
-                both = turn.tile([P, QT, 2, HALF], F32, name="th", tag="v0")
-                for i in range(QT):
-                    th[i] = both[:, i, :, :]
-            nc.scalar.activation(th[a][:, h, :], s_tp[a, h][:], ACT.Tanh, scale=0.5)
+            nc.scalar.activation(capped[a, h], score_bank[a, h][:], ACT.Tanh, scale=0.5)
 
-        def row_max(a, h):
-            if not nmx:
-                t = turn.tile([P, 2 * QT], F32, name="nmx", tag="turn")
-                for i in range(2 * QT):
-                    nmx[i // 2, i % 2] = t[:, i : i + 1]
-            nc.vector.tensor_reduce(nmx[a, h], th[a][:, h, :], AX.X, ALU.max, negate=True)
+        scale_bank = {}
+        scale_column = {}
 
-        vs_g = {}
-        vs_t = {}
+        def turn_scales(h):
+            bank = psum_slots.tile([P, PACK, P], F32, name="slot_bank")
+            for t in range(PACK):
+                first = h * PASS + t
+                nc.tensor.transpose(bank[:, t, :], vs_gathered[:, first : (h + 1) * PASS : PACK], ident[:])
+            scale_bank[h] = bank
 
-        vs_tp = {}
+        def pick_scales(h):
+            scale_column[h] = keep.tile([P, PACK], F32, name=f"scale_column{h}")
+            nc.vector.tensor_copy(scale_column[h][:], scale_bank[h][:, :, 0])
 
-        def gather_vs():
-            g = keep.tile([P, N], F32, name="vs_g")
-            nc.vector.tensor_copy(g[:], shared["vs"][:].indirect(offsets[:]))
-            for h in range(2):
-                vs_g[h] = g[:, h * HALF : (h + 1) * HALF]
-
-        def turn_vs(h):
-            vs_tp[h] = psum_v.tile([P, 4, P], F32, name="tv")
-            for t in range(4):
-                nc.tensor.transpose(vs_tp[h][:, t, :], vs_g[h][:, t:HALF:4], ident[:])
-
-        def column_vs(h):
-            vs_t[h] = keep.tile([P, 4], F32, name=f"vs_t{h}")
-            nc.vector.tensor_copy(vs_t[h][:], vs_tp[h][:, :, 0])
-
-        v_codes = {}
-        v_scales = {}
-
-        v_g = {}
-        v_tp = {}
-        v_bf = {}
-
-        def gather_v(h):
-            v_g[h] = keep.tile([P, HALF], U32, name=f"v_g{h}")
-            dst = v_g[h][:].rearrange("p (t s) -> p s t", t=4)
-            nc.vector.tensor_copy(dst, v_win.indirect(halves[h]))
-
-        def turn_v(h):
-            v_tp[h] = psum_v.tile([P, 4, P], F32, name="tv")
-            v_words = v_g[h][:].bitcast(F32)
-            for t in range(4):
-                nc.tensor.transpose(v_tp[h][:, t, :], v_words[:, t * P : (t + 1) * P], ident[:])
-
-        def evac_v(h):
-            v_bf[h] = keep.tile([P, DV, 4], BF16, name=f"v_bf{h}", align_bytes=64)
-            src = v_tp[h][:].rearrange("p t w -> p (t w)").bitcast(BF16).rearrange("p (t e) -> p e t", t=4)
-            nc.scalar.copy(v_bf[h][:], src)
-
-        def quant_v(h):
-            c = keep.tile([P, DV], U32, name=f"v_codes{h}", align_bytes=64)
-            s = keep.tile([P, DV], U8, name=f"v_scales{h}", align_bytes=64)
-            quantize(c[:], s[:], v_bf[h][:])
-            v_codes[h] = c
-            v_scales[h] = s
-
-        neg_m = {}
+        neg_max = []
 
         def finish_max(a):
-            nm = keep.tile([P, 1], F32, name=f"neg_m{a}")
-            nc.vector.tensor_scalar(nm[:], nmx[a, 0], nmx[a, 1], 2.0, ALU.min, ALU.mult)
-            neg_m[a] = nm
+            tile = keep.tile([P, 1], F32, name=f"neg_max{a}")
+            first, second = (neg_half_max[:, HALVES * a + h : HALVES * a + h + 1] for h in range(HALVES))
+            nc.vector.tensor_scalar(tile[:], first, second, 2.0, ALU.min, ALU.mult)
+            neg_max.append(tile)
 
-        w_codes = {}
-        w_scales = {}
-        sums = {}
-        p_t = {}
+        v_bank = {}
+        v_grouped = {}
+        v_packed = {}
 
-        def weights_exp(a, h):
-            if not p_t:
-                every = turn.tile([P, QT, 2, HALF], F32, name="p", tag="v1")
-                for i in range(2 * QT):
-                    p_t[i // 2, i % 2] = every[:, i // 2, i % 2, :]
-            p = p_t[a, h]
-            l_t = keep.tile([P, 1], F32, name=f"l{a}{h}")
-            nc.scalar.activation(p, th[a][:, h, :], ACT.Exp, bias=neg_m[a][:], scale=2.0, accum_out=l_t[:])
-            sums[a, h] = l_t
+        def gather_values(h):
+            dst = v_words[:, h * PASS : (h + 1) * PASS].rearrange("p (t s) -> p s t", t=PACK)
+            nc.vector.tensor_copy(dst, window[VALUES].indirect(slots[h]))
 
-        w_tp = {}
-        w_bf = {}
+        def turn_values(h):
+            bank = psum_slots.tile([P, PACK, P], F32, name="slot_bank")
+            words = v_words[:].bitcast(F32)
+            for t in range(PACK):
+                first = h * PASS + t * P
+                nc.tensor.transpose(bank[:, t, :], words[:, first : first + P], ident[:])
+            v_bank[h] = bank
 
-        def turn_w(a, h):
-            w_tp[a, h] = psum_t.tile([P, 4, P], F32, name="tp")
-            for t in range(4):
-                nc.tensor.transpose(w_tp[a, h][:, t, :], p_t[a, h][:, t * P : (t + 1) * P], ident[:])
+        def group_values(h):
+            v_grouped[h] = keep.tile([P, DV, PACK], BF16, name=f"v_grouped{h}", align_bytes=64)
+            src = v_bank[h][:].rearrange("p t w -> p (t w)").bitcast(BF16)
+            nc.scalar.copy(v_grouped[h][:], src.rearrange("p (t e) -> p e t", t=PACK))
 
-        def scale_w(a, h):
-            w_bf[a, h] = keep.tile([P, P, 4], BF16, name=f"w_bf{a}{h}", align_bytes=64)
+        def quantize_values(h):
+            v_packed[h] = packed(DV, f"v{h}")
+            quantize(v_packed[h][0][:], v_packed[h][1][:], v_grouped[h][:])
+
+        w_bank = {}
+        w_grouped = {}
+        w_packed = {}
+
+        def turn_weights(a, h):
+            bank = psum_weights.tile([P, PACK, P], F32, name="weight_bank")
+            for t in range(PACK):
+                nc.tensor.transpose(bank[:, t, :], exps[:, a, h, t * P : (t + 1) * P], ident[:])
+            w_bank[a, h] = bank
+
+        def scale_weights(a, h):
+            w_grouped[a, h] = keep.tile([P, P, PACK], BF16, name=f"w_grouped{a}{h}", align_bytes=64)
             nc.vector.tensor_tensor(
-                w_bf[a, h][:],
-                w_tp[a, h][:].rearrange("p t q -> p q t"),
-                vs_t[h][:].unsqueeze(1).to_broadcast([P, P, 4]),
+                w_grouped[a, h][:],
+                w_bank[a, h][:].rearrange("p t q -> p q t"),
+                scale_column[h][:].unsqueeze(1).to_broadcast([P, P, PACK]),
                 ALU.mult,
             )
 
-        def quant_w(a, h):
-            c = keep.tile([P, P], U32, name=f"w_codes{a}{h}", align_bytes=64)
-            s = keep.tile([P, P], U8, name=f"w_scales{a}{h}", align_bytes=64)
-            quantize(c[:], s[:], w_bf[a, h][:])
-            w_codes[a, h] = c
-            w_scales[a, h] = s
+        def quantize_weights(a, h):
+            w_packed[a, h] = packed(P, f"w{a}{h}")
+            quantize(w_packed[a, h][0][:], w_packed[a, h][1][:], w_grouped[a, h][:])
 
-        gate_t = {}
-        gate = {}
+        y_bank = {}
 
-        def do_gate():
-            g = turn.tile([P, QT, DV], F32, name="gate_t", tag="v0")
-            nc.scalar.activation(g[:], og_raw[:], ACT.Tanh, scale=0.5)
-            for a in range(QT):
-                gate_t[a] = g[:, a, :]
-
-        r_l = {}
-        y_tp = {}
-
-        def inverse_sum(a):
-            l_sum = keep.tile([P, 1], F32, name=f"l_sum{a}")
-            nc.vector.tensor_scalar(l_sum[:], sums[a, 0][:], sums[a, 1][:], 2.0, ALU.add, ALU.mult)
-            r_l[a] = keep.tile([P, 1], F32, name=f"r_l{a}")
-            nc.vector.reciprocal(r_l[a][:], l_sum[:])
-
-        def scale_gate(a):
-            gate[a] = keep.tile([P, DV], F32, name=f"gate{a}")
-            nc.scalar.activation(gate[a][:], gate_t[a], ACT.Identity, bias=r_l[a][:], scale=r_l[a][:])
-
-        def product(a):
-            y_ps = psum_s.tile([P, HALF], F32, name="s_ps")
-            for h in range(2):
+        def weigh_values(a):
+            bank = psum_scores.tile([P, PASS], F32, name="score_bank")
+            for h in range(HALVES):
                 nc.tensor.matmul_mx(
-                    out=y_ps[:, 0:DV],
-                    lhsT=w_codes[a, h][:].bitcast(FP8X4),
-                    lhsT_scale=w_scales[a, h][:],
-                    rhs=v_codes[h][:].bitcast(FP8X4),
-                    rhs_scale=v_scales[h][:],
+                    out=bank[:, 0:DV],
+                    lhsT=w_packed[a, h][0][:].bitcast(FP8X4),
+                    lhsT_scale=w_packed[a, h][1][:],
+                    rhs=v_packed[h][0][:].bitcast(FP8X4),
+                    rhs_scale=v_packed[h][1][:],
                     start=(h == 0),
-                    stop=(h == 1),
+                    stop=(h == HALVES - 1),
                 )
-            y_tp[a] = y_ps
+            y_bank[a] = bank
 
-        def finish(a):
-            y_ps = y_tp[a]
-            o = keep.tile([P, DV], F32, name=f"o{a}")
-            nc.vector.tensor_tensor(o[:], y_ps[:, 0:DV], gate[a][:], ALU.mult)
-            nc.sync.dma_start(out[0, a * P : (a + 1) * P, :], o[:])
+        for piece in CASTS[KEYS_LOW]:
+            cast(KEYS_LOW, *piece)
+        for h in range(HALVES):
+            gather_keys(KEYS_LOW, h)
+        for piece in CASTS[KEYS_HIGH]:
+            cast(KEYS_HIGH, *piece)
+        for h in range(HALVES):
+            gather_keys(KEYS_HIGH, h)
+        quantize_keys(0)
+        q_grouped = keep.tile([P, NQ, PACK], BF16, name="q_grouped", align_bytes=64)
+        q_packed = packed(NQ, "q")
+        nc.scalar.activation(q_grouped[:], q_raw[:].rearrange("p j w -> p w j"), ACT.Copy)
+        quantize(q_packed[0][:], q_packed[1][:], q_grouped[:])
+        quantize_keys(1)
 
-        load(0, 0)
-        load(0, 1)
-        load(1, 0)
-        load(1, 1)
-        load_q()
-        load(2, 0)
-        load_vs()
-        load(2, 1)
-        load_og()
-        cast_piece(0, 0, 512, "S")
-        cast_piece(0, 512, 512, "S")
-        cast_piece(0, 1024, 512, "S")
-        cast_piece(0, 1536, 512, "V")
-        gather_k(0, 0)
-        gather_k(0, 1)
-        cast_piece(1, 0, 512, "S")
-        cast_piece(1, 512, 512, "V")
-        cast_piece(1, 1024, 384, "S")
-        cast_piece(1, 1408, 640, "V")
-        gather_k(1, 0)
-        gather_k(1, 1)
-        quantize(k_codes[0][:], k_scales[0][:], k_gath[0][:])
-        cast_q()
-        quantize(q_codes[:], q_scales[:], q_bf[:])
-        quantize(k_codes[1][:], k_scales[1][:], k_gath[1][:])
-        cast_piece(2, 0, 512, "S")
-        cast_piece(2, 512, 512, "S")
-        gather_vs()
-        score(0, 0)
-        cap(0, 0)
-        score(1, 0)
-        cap(1, 0)
-        score(0, 1)
-        cap(0, 1)
-        score(1, 1)
-        cap(1, 1)
-        cast_piece(2, 1024, 640, "S")
-        cast_piece(2, 1664, 384, "V")
-        turn_vs(0)
-        turn_vs(1)
-        row_max(0, 0)
-        row_max(0, 1)
-        finish_max(0)
-        row_max(1, 0)
-        row_max(1, 1)
-        finish_max(1)
-        weights_exp(0, 0)
-        weights_exp(0, 1)
-        weights_exp(1, 0)
-        weights_exp(1, 1)
-        column_vs(0)
-        column_vs(1)
-        gather_v(0)
-        turn_v(0)
-        evac_v(0)
-        gather_v(1)
-        turn_v(1)
-        evac_v(1)
-        quant_v(0)
-        quant_v(1)
-        turn_w(0, 0)
-        turn_w(0, 1)
-        scale_w(0, 0)
-        scale_w(0, 1)
-        quant_w(0, 0)
-        quant_w(0, 1)
-        turn_w(1, 0)
-        scale_w(1, 0)
-        quant_w(1, 0)
-        turn_w(1, 1)
-        scale_w(1, 1)
-        quant_w(1, 1)
-        product(0)
-        product(1)
-        do_gate()
-        inverse_sum(0)
-        scale_gate(0)
-        inverse_sum(1)
-        scale_gate(1)
-        finish(0)
-        finish(1)
+        for piece in CASTS[VALUES][:2]:
+            cast(VALUES, *piece)
+        vs_gathered = keep.tile([P, N], F32, name="vs_gathered")
+        nc.vector.tensor_copy(vs_gathered[:], vs_raw[:].indirect(offsets[:]))
+        tanhs = handover.tile([P, QT, HALVES, PASS], F32, name="tanhs", tag="values0")
+        for a in range(QT):
+            for h in range(HALVES):
+                capped[a, h] = tanhs[:, a, h, :]
+        for h in range(HALVES):
+            for a in range(QT):
+                score(a, h)
+                cap(a, h)
+
+        for piece in CASTS[VALUES][2:]:
+            cast(VALUES, *piece)
+        for h in range(HALVES):
+            turn_scales(h)
+        neg_half_max = handover.tile([P, QT * HALVES], F32, name="neg_half_max", tag="scales")
+        for a in range(QT):
+            for h in range(HALVES):
+                column = HALVES * a + h
+                nc.vector.tensor_reduce(
+                    neg_half_max[:, column : column + 1], capped[a, h], AX.X, ALU.max, negate=True
+                )
+            finish_max(a)
+        exps = handover.tile([P, QT, HALVES, PASS], F32, name="exps", tag="values1")
+        sums = keep.tile([P, QT, HALVES], F32, name="sums")
+        for a in range(QT):
+            for h in range(HALVES):
+                nc.scalar.activation(
+                    exps[:, a, h, :],
+                    capped[a, h],
+                    ACT.Exp,
+                    bias=neg_max[a][:],
+                    scale=2.0,
+                    accum_out=sums[:, a, h : h + 1],
+                )
+        for h in range(HALVES):
+            pick_scales(h)
+
+        v_words = handover.tile([P, N], U32, name="v_words", tag="scales")
+        for h in range(HALVES):
+            gather_values(h)
+            turn_values(h)
+            group_values(h)
+        for h in range(HALVES):
+            quantize_values(h)
+        for a in range(QT):
+            for h in range(HALVES):
+                turn_weights(a, h)
+                scale_weights(a, h)
+                quantize_weights(a, h)
+
+        for a in range(QT):
+            weigh_values(a)
+        gate_tanh = handover.tile([P, QT, DV], F32, name="gate_tanh", tag="values0")
+        nc.scalar.activation(gate_tanh[:], og_raw[:], ACT.Tanh, scale=0.5)
+        gate = keep.tile([P, QT, DV], F32, name="gate")
+        nc.scalar.activation(gate[:], gate_tanh[:], ACT.Identity, bias=half[:], scale=0.5)
+        row_sum = keep.tile([P, QT], F32, name="row_sum")
+        nc.vector.tensor_tensor(row_sum[:], sums[:, :, 0], sums[:, :, 1], ALU.add)
+        inverse = keep.tile([P, QT], F32, name="inverse")
+        nc.vector.reciprocal(inverse[:], row_sum[:])
+        for a in range(QT):
+            result = keep.tile([P, DV], F32, name=f"result{a}")
+            nc.vector.scalar_tensor_tensor(
+                result[:],
+                y_bank[a][:, 0:DV],
+                inverse[:, a : a + 1],
+                gate[:, a, :],
+                ALU.mult,
+                ALU.mult,
+            )
+            nc.sync.dma_start(out[0, a * P : (a + 1) * P, :], result[:])

from contextlib import ExitStack

import concourse.mybir as mybir
from concourse.masks import make_identity

P = 128
NQ, D, DV, T, N = 256, 512, 256, 2048, 1024
PACK = 4
PASS = P * PACK
HALVES = N // PASS
QT = NQ // P
FLOPS = 2 * NQ * N * (D + DV)

F32 = mybir.dt.float32
BF16 = mybir.dt.bfloat16
U32 = mybir.dt.uint32
U16 = mybir.dt.uint16
U8 = mybir.dt.uint8
FP8X4 = mybir.dt.float8_e4m3fn_x4
ACT = mybir.ActivationFunctionType
ALU = mybir.AluOpType
AX = mybir.AxisListType

KEYS_LOW, KEYS_HIGH, VALUES = 0, 1, 2
KEY_LOADS = (
    (KEYS_LOW, 0, 1024),
    (KEYS_LOW, 1024, 1024),
    (KEYS_HIGH, 0, 1024),
    (KEYS_HIGH, 1024, 768),
    (KEYS_HIGH, 1792, 256),
)
CASTS = {
    KEYS_LOW: ((0, 512, True), (512, 512, True), (1024, 448, True), (1472, 576, False)),
    KEYS_HIGH: (
        (0, 512, True),
        (512, 512, True),
        (1024, 320, True),
        (1344, 448, False),
        (1792, 256, False),
    ),
    VALUES: ((0, 512, True), (512, 512, True), (1024, 640, True), (1664, 384, False)),
}


def tile_attend_x_cap_gate_topk_kernel(tc, qT, kT, vT, vs, og, offs, out):
    nc = tc.nc
    with ExitStack() as ctx:
        keep = ctx.enter_context(tc.tile_pool(name="keep", bufs=1))
        handover = ctx.enter_context(tc.tile_pool(name="handover", bufs=1))
        psum_scores = ctx.enter_context(tc.psum_pool(name="psum_scores", bufs=3))
        psum_weights = ctx.enter_context(tc.psum_pool(name="psum_weights", bufs=3))
        psum_slots = ctx.enter_context(tc.psum_pool(name="psum_slots", bufs=2))

        half = keep.tile([P, 1], F32, name="half")
        nc.gpsimd.memset(half[:], 0.5)
        warm = keep.tile([P, 1], F32, name="warm")
        nc.scalar.activation(warm[:], half[:], ACT.Exp)
        ident = keep.tile([P, P], F32, name="ident")
        make_identity(nc, ident[:])

        k_rows = kT.rearrange("(p j) w -> p j w", j=PACK)
        v_rows = vT.rearrange("(p j) w -> p j w", j=2)
        raw = {}

        def load(pair, c0, cw, tag=None):
            rows = v_rows if pair == VALUES else k_rows[:, 2 * pair : 2 * pair + 2, :]
            name = f"raw{pair}_{c0}"
            if tag is None:
                tile = keep.tile([P, 2, cw], F32, name=name)
            else:
                tile = handover.tile([P, 2, cw], F32, name=name, tag=tag)
            nc.sync.dma_start(tile[:], rows[:, :, c0 : c0 + cw])
            raw[pair, c0] = tile

        offsets = keep.tile([P, N // 16], U16, name="offsets")
        load(*KEY_LOADS[0])
        nc.sync.dma_start(offsets[:], offs)
        for each in KEY_LOADS[1:]:
            load(*each)
        q_raw = keep.tile([P, PACK, NQ], F32, name="q_raw")
        nc.sync.dma_start(q_raw[:], qT[0].rearrange("(p j) w -> p j w", j=PACK))
        load(VALUES, 0, T // 2, tag="values0")
        vs_raw = handover.tile([P, T], F32, name="vs_raw", tag="scales")
        nc.sync.dma_start(vs_raw[:], vs)
        load(VALUES, T // 2, T // 2, tag="values1")
        og_raw = keep.tile([P, QT, DV], F32, name="og_raw")
        nc.sync.dma_start(og_raw[:], og[0].rearrange("(a p) e -> p a e", p=P))

        columns = PASS // 16
        slots = [offsets[:, h * columns : (h + 1) * columns] for h in range(HALVES)]

        paired = []
        window = []
        for pair in (KEYS_LOW, KEYS_HIGH, VALUES):
            tile = keep.tile([P, T, 2], BF16, name=f"paired{pair}")
            paired.append(tile)
            window.append(tile[:].rearrange("p w j -> p (w j)").bitcast(U32))

        def cast(pair, c0, cw, on_scalar):
            start = max(s for owner, s in raw if owner == pair and s <= c0)
            src = raw[pair, start][:, :, c0 - start : c0 - start + cw].rearrange("p j w -> p w j")
            dst = paired[pair][:, c0 : c0 + cw, :]
            if on_scalar:
                nc.scalar.activation(dst, src, ACT.Copy)
            else:
                nc.vector.tensor_copy(dst, src)

        def quantize(codes, scales, grouped):
            nc.vector.quantize_mx(
                out=codes.bitcast(FP8X4), scales=scales, in_=grouped.rearrange("p n t -> p (n t)")
            )

        def packed(width, name):
            codes = keep.tile([P, width], U32, name=f"{name}_codes", align_bytes=64)
            scales = keep.tile([P, width], U8, name=f"{name}_scales", align_bytes=64)
            return codes, scales

        k_grouped = []
        for h in range(HALVES):
            k_grouped.append(keep.tile([P, PASS, PACK], BF16, name=f"k_grouped{h}", align_bytes=64))
        k_packed = [packed(PASS, f"k{h}") for h in range(HALVES)]

        def gather_keys(pair, h):
            words = k_grouped[h][:].rearrange("p n t -> p (n t)").bitcast(U32)
            by_slot = words.rearrange("p (t s u) -> p s t u", t=PACK, u=2)
            nc.vector.tensor_copy(by_slot[:, :, :, pair], window[pair].indirect(slots[h]))

        def quantize_keys(h):
            quantize(k_packed[h][0][:], k_packed[h][1][:], k_grouped[h][:])

        score_bank = {}
        capped = {}

        def score(a, h):
            q_cols = slice(a * P, (a + 1) * P)
            bank = psum_scores.tile([P, PASS], F32, name="score_bank")
            nc.tensor.matmul_mx(
                out=bank[:],
                lhsT=q_packed[0][:, q_cols].bitcast(FP8X4),
                lhsT_scale=q_packed[1][:, q_cols],
                rhs=k_packed[h][0][:].bitcast(FP8X4),
                rhs_scale=k_packed[h][1][:],
                start=True,
                stop=True,
            )
            score_bank[a, h] = bank

        def cap(a, h):
            nc.scalar.activation(capped[a, h], score_bank[a, h][:], ACT.Tanh, scale=0.5)

        scale_bank = {}
        scale_column = {}

        def turn_scales(h):
            bank = psum_slots.tile([P, PACK, P], F32, name="slot_bank")
            for t in range(PACK):
                first = h * PASS + t
                nc.tensor.transpose(bank[:, t, :], vs_gathered[:, first : (h + 1) * PASS : PACK], ident[:])
            scale_bank[h] = bank

        def pick_scales(h):
            scale_column[h] = keep.tile([P, PACK], F32, name=f"scale_column{h}")
            nc.vector.tensor_copy(scale_column[h][:], scale_bank[h][:, :, 0])

        neg_max = []

        def finish_max(a):
            tile = keep.tile([P, 1], F32, name=f"neg_max{a}")
            first, second = (neg_half_max[:, HALVES * a + h : HALVES * a + h + 1] for h in range(HALVES))
            nc.vector.tensor_scalar(tile[:], first, second, 2.0, ALU.min, ALU.mult)
            neg_max.append(tile)

        v_bank = {}
        v_grouped = {}
        v_packed = {}

        def gather_values(h):
            dst = v_words[:, h * PASS : (h + 1) * PASS].rearrange("p (t s) -> p s t", t=PACK)
            nc.vector.tensor_copy(dst, window[VALUES].indirect(slots[h]))

        def turn_values(h):
            bank = psum_slots.tile([P, PACK, P], F32, name="slot_bank")
            words = v_words[:].bitcast(F32)
            for t in range(PACK):
                first = h * PASS + t * P
                nc.tensor.transpose(bank[:, t, :], words[:, first : first + P], ident[:])
            v_bank[h] = bank

        def group_values(h):
            v_grouped[h] = keep.tile([P, DV, PACK], BF16, name=f"v_grouped{h}", align_bytes=64)
            src = v_bank[h][:].rearrange("p t w -> p (t w)").bitcast(BF16)
            nc.scalar.copy(v_grouped[h][:], src.rearrange("p (t e) -> p e t", t=PACK))

        def quantize_values(h):
            v_packed[h] = packed(DV, f"v{h}")
            quantize(v_packed[h][0][:], v_packed[h][1][:], v_grouped[h][:])

        w_bank = {}
        w_grouped = {}
        w_packed = {}

        def turn_weights(a, h):
            bank = psum_weights.tile([P, PACK, P], F32, name="weight_bank")
            for t in range(PACK):
                nc.tensor.transpose(bank[:, t, :], exps[:, a, h, t * P : (t + 1) * P], ident[:])
            w_bank[a, h] = bank

        def scale_weights(a, h):
            w_grouped[a, h] = keep.tile([P, P, PACK], BF16, name=f"w_grouped{a}{h}", align_bytes=64)
            nc.vector.tensor_tensor(
                w_grouped[a, h][:],
                w_bank[a, h][:].rearrange("p t q -> p q t"),
                scale_column[h][:].unsqueeze(1).to_broadcast([P, P, PACK]),
                ALU.mult,
            )

        def quantize_weights(a, h):
            w_packed[a, h] = packed(P, f"w{a}{h}")
            quantize(w_packed[a, h][0][:], w_packed[a, h][1][:], w_grouped[a, h][:])

        y_bank = {}

        def weigh_values(a):
            bank = psum_scores.tile([P, PASS], F32, name="score_bank")
            for h in range(HALVES):
                nc.tensor.matmul_mx(
                    out=bank[:, 0:DV],
                    lhsT=w_packed[a, h][0][:].bitcast(FP8X4),
                    lhsT_scale=w_packed[a, h][1][:],
                    rhs=v_packed[h][0][:].bitcast(FP8X4),
                    rhs_scale=v_packed[h][1][:],
                    start=(h == 0),
                    stop=(h == HALVES - 1),
                )
            y_bank[a] = bank

        for piece in CASTS[KEYS_LOW]:
            cast(KEYS_LOW, *piece)
        for h in range(HALVES):
            gather_keys(KEYS_LOW, h)
        for piece in CASTS[KEYS_HIGH]:
            cast(KEYS_HIGH, *piece)
        for h in range(HALVES):
            gather_keys(KEYS_HIGH, h)
        quantize_keys(0)
        q_grouped = keep.tile([P, NQ, PACK], BF16, name="q_grouped", align_bytes=64)
        q_packed = packed(NQ, "q")
        nc.scalar.activation(q_grouped[:], q_raw[:].rearrange("p j w -> p w j"), ACT.Copy)
        quantize(q_packed[0][:], q_packed[1][:], q_grouped[:])
        quantize_keys(1)

        for piece in CASTS[VALUES][:2]:
            cast(VALUES, *piece)
        vs_gathered = keep.tile([P, N], F32, name="vs_gathered")
        nc.vector.tensor_copy(vs_gathered[:], vs_raw[:].indirect(offsets[:]))
        tanhs = handover.tile([P, QT, HALVES, PASS], F32, name="tanhs", tag="values0")
        for a in range(QT):
            for h in range(HALVES):
                capped[a, h] = tanhs[:, a, h, :]
        for h in range(HALVES):
            for a in range(QT):
                score(a, h)
                cap(a, h)

        for piece in CASTS[VALUES][2:]:
            cast(VALUES, *piece)
        for h in range(HALVES):
            turn_scales(h)
        neg_half_max = handover.tile([P, QT * HALVES], F32, name="neg_half_max", tag="scales")
        for a in range(QT):
            for h in range(HALVES):
                column = HALVES * a + h
                nc.vector.tensor_reduce(
                    neg_half_max[:, column : column + 1], capped[a, h], AX.X, ALU.max, negate=True
                )
            finish_max(a)
        exps = handover.tile([P, QT, HALVES, PASS], F32, name="exps", tag="values1")
        sums = keep.tile([P, QT, HALVES], F32, name="sums")
        for a in range(QT):
            for h in range(HALVES):
                nc.scalar.activation(
                    exps[:, a, h, :],
                    capped[a, h],
                    ACT.Exp,
                    bias=neg_max[a][:],
                    scale=2.0,
                    accum_out=sums[:, a, h : h + 1],
                )
        for h in range(HALVES):
            pick_scales(h)

        v_words = handover.tile([P, N], U32, name="v_words", tag="scales")
        for h in range(HALVES):
            gather_values(h)
            turn_values(h)
            group_values(h)
        for h in range(HALVES):
            quantize_values(h)
        for a in range(QT):
            for h in range(HALVES):
                turn_weights(a, h)
                scale_weights(a, h)
                quantize_weights(a, h)

        for a in range(QT):
            weigh_values(a)
        gate_tanh = handover.tile([P, QT, DV], F32, name="gate_tanh", tag="values0")
        nc.scalar.activation(gate_tanh[:], og_raw[:], ACT.Tanh, scale=0.5)
        gate = keep.tile([P, QT, DV], F32, name="gate")
        nc.scalar.activation(gate[:], gate_tanh[:], ACT.Identity, bias=half[:], scale=0.5)
        row_sum = keep.tile([P, QT], F32, name="row_sum")
        nc.vector.tensor_tensor(row_sum[:], sums[:, :, 0], sums[:, :, 1], ALU.add)
        inverse = keep.tile([P, QT], F32, name="inverse")
        nc.vector.reciprocal(inverse[:], row_sum[:])
        for a in range(QT):
            result = keep.tile([P, DV], F32, name=f"result{a}")
            nc.vector.scalar_tensor_tensor(
                result[:],
                y_bank[a][:, 0:DV],
                inverse[:, a : a + 1],
                gate[:, a, :],
                ALU.mult,
                ALU.mult,
            )
            nc.sync.dma_start(out[0, a * P : (a + 1) * P, :], result[:])
